import numpy as np
import ml_dtypes


def mxq(x, axis, fmt="e4m3"):
    dtype, down = {"e4m3": (ml_dtypes.float8_e4m3fn, 7), "e5m2": (ml_dtypes.float8_e5m2, 14)}[fmt]
    v = np.moveaxis(np.asarray(x, np.float32).astype(ml_dtypes.bfloat16).astype(np.float64), axis, -1)
    blocks = v.reshape(v.shape[:-1] + (-1, 32))
    amax = np.abs(blocks).max(-1, keepdims=True)
    byte = np.maximum(np.where(amax > 0, np.frexp(amax)[1] - 1 + 127, 0) - down, 1)
    scale = np.exp2(byte - 127.0)
    codes = (blocks / scale).astype(np.float32).astype(dtype).astype(np.float64)
    return np.moveaxis((codes * scale).reshape(v.shape), -1, axis)


WIDE = False


def mx_kscale(k):
    if not WIDE:
        return np.ones(k)
    levels = np.array([10, -10, 5, -5, 0])
    if k % 512:
        return np.exp2(np.random.permutation(np.resize(levels, k // 32))).repeat(32)
    a = np.empty((k // 512, 16))
    for p in range(k // 512):
        a[p, :8] = np.random.permutation(np.resize(levels, 8))
        for g in range(8):
            far = levels[np.abs(levels - a[p, g]) >= 10]
            a[p, g + 8] = far[np.random.randint(len(far))]
    return np.exp2(a.ravel()).repeat(32)


def f64(x):
    return np.asarray(x).astype(np.float64)


def striped(idx):
    return np.tile(idx.reshape(-1, 16).T, (8, 1)).astype(np.uint16)


def unstriped(offs):
    return offs[:16].T.reshape(-1).astype(np.int64)


E2M1 = np.array([0.0, 0.5, 1.0, 1.5, 2.0, 3.0, 4.0, 6.0, -0.0, -0.5, -1.0, -1.5, -2.0, -3.0, -4.0, -6.0])


def pack_weight(w, fmt):
    k, n = w.shape
    w = f64(np.asarray(w, np.float32).astype(ml_dtypes.bfloat16)).reshape(k // 32, 32, n)
    amax = np.abs(w).max(1)
    if fmt == "e4m3":
        byte = np.frexp(amax)[1] - 1 + 127 - 7
    else:
        mant, ex = np.frexp(amax / 6.0)
        byte = np.where(mant > 0.5, ex, ex - 1) + 127
    byte = np.clip(np.where(amax > 0, byte, 1), 1, 254)
    scaled = (w * np.exp2(127.0 - byte)[:, None, :]).reshape(k, n).astype(np.float32)
    by_word = np.ascontiguousarray(scaled.reshape(k // 512, 128, 4, n).transpose(0, 1, 3, 2))
    if fmt == "e4m3":
        words = by_word.astype(ml_dtypes.float8_e4m3fn).view(np.uint8)
    else:
        c = by_word.astype(ml_dtypes.float4_e2m1fn).view(np.uint8) & 0xF
        words = (c[..., 0::2] | (c[..., 1::2] << 4)).reshape(k // 512, 128, 2 * n)
    return np.ascontiguousarray(words), np.ascontiguousarray(byte.astype(np.uint8).reshape(k // 512, 16, n))


def unpack_weight(words, scales, fmt):
    g, _, n = scales.shape
    words = np.ascontiguousarray(words).reshape(g, 128, n, -1)
    if fmt == "e4m3":
        vals = words.view(ml_dtypes.float8_e4m3fn).astype(np.float64)
    else:
        nib = np.empty((g, 128, n, 4), np.uint8)
        nib[..., 0::2] = words & 0xF
        nib[..., 1::2] = words >> 4
        vals = E2M1[nib]
    vals = vals * np.repeat(np.exp2(scales.astype(np.float64) - 127.0), 8, axis=1)[..., None]
    return vals.transpose(0, 1, 3, 2).reshape(g * 512, n)


def gelu(v):
    return 0.5 * v * (1.0 + np.tanh(np.sqrt(2.0 / np.pi) * (v + 0.044715 * v**3)))


K, M, T, S, P, H, N, T2 = 1024, 512, 2048, 1024, 512, 1024, 512, 2048

def setup_inputs():
    n = np.random.standard_normal
    s1 = mx_kscale(K)[:, None]
    s2 = mx_kscale(M)[:, None]
    u = mx_kscale(H)[:, None]
    tab_words, tab_scales = pack_weight(n((K, T)) * s1, "e4m3")
    tab2_words, tab2_scales = pack_weight(n((M, T)) * s2, "e4m3")
    w2_words, w2_scales = pack_weight(n((M, H)) / np.sqrt(M) / s2, "e2m1")
    w3_words, w3_scales = pack_weight(n((H, N)) / np.sqrt(H) / u, "e2m1")
    perm = np.random.permutation(T2)
    return {"tab_words": tab_words, "tab_scales": tab_scales,
            "tab2_words": tab2_words, "tab2_scales": tab2_scales,
            "offs": striped(np.random.permutation(T)[:S]), "offs2": striped(np.random.permutation(T)[:P]),
            "pos1": striped(np.random.permutation(S)[:P]),
            "offs3": striped(perm[:S]), "offs4": striped(perm[S:S + P]),
            "w1": (n((K, H)) / np.sqrt(K) / s1).astype(np.float32),
            "w2_words": w2_words, "w2_scales": w2_scales,
            "gain1": (np.exp(0.3 * n(H)) * u[:, 0]).astype(np.float32),
            "gain2": (np.exp(0.3 * n(H)) * u[:, 0]).astype(np.float32),
            "w3_words": w3_words, "w3_scales": w3_scales,
            "w4": (n((H, N)) / np.sqrt(H) / u).astype(np.float32),
            "wg1": np.exp(0.3 * n((128, S))).astype(np.float32),
            "wg2": np.exp(0.3 * n((128, P))).astype(np.float32),
            "page1": n((N, T2)).astype(np.float32)}

def reference(tab_words, tab_scales, tab2_words, tab2_scales, offs, offs2, pos1, offs3, offs4, w1, w2_words, w2_scales, gain1, gain2, w3_words, w3_scales, w4, wg1, wg2, page1):
    v = unpack_weight(tab_words, tab_scales, "e4m3")[:, unstriped(offs)]
    v2 = unpack_weight(tab2_words, tab2_scales, "e4m3")[:, unstriped(offs2)]
    h1 = mxq(f64(w1), 0, "e4m3").T @ v
    h2 = unpack_weight(w2_words, w2_scales, "e2m1").T @ v2
    z1 = np.square(h1) * f64(gain1)[:, None]
    z2 = (h2 + h1[:, unstriped(pos1)]) * h2 * f64(gain2)[:, None]
    y1 = unpack_weight(w3_words, w3_scales, "e2m1").T @ mxq(z1, 0, "e4m3")
    y2 = mxq(f64(w4), 0, "e4m3").T @ mxq(z2, 0, "e4m3")
    out = f64(page1).copy()
    out[:, unstriped(offs3)] = np.tile(f64(wg1), (N // 128, 1)) * y1
    out[:, unstriped(offs4)] = np.tile(f64(wg2), (N // 128, 1)) * y2
    return out

@@ -1,0 +1,351 @@
+from contextlib import ExitStack
+
+import concourse.mybir as mybir
+
+K, M, T, S, C, H, N, T2 = 1024, 512, 2048, 1024, 512, 1024, 512, 2048
+FLOPS = 2 * (K * H * S + M * H * C + H * N * S + H * N * C)
+
+F32 = mybir.dt.float32
+BF16 = mybir.dt.bfloat16
+I32 = mybir.dt.int32
+U32 = mybir.dt.uint32
+U16 = mybir.dt.uint16
+U8 = mybir.dt.uint8
+FP8X4 = mybir.dt.float8_e4m3fn_x4
+FP4X4 = mybir.dt.float4_e2m1fn_x4
+MULT = mybir.AluOpType.mult
+ADD = mybir.AluOpType.add
+COPY = mybir.ActivationFunctionType.Copy
+SQUARE = mybir.ActivationFunctionType.Square
+
+P = 128
+PACK = 4
+PASS = P * PACK
+BANK = 512
+CHUNK = 256
+
+
+def tile_list_credit_discrepancy_page_kernel(
+    tc, tab_words, tab_scales, tab2_words, tab2_scales, offs, offs2, pos1, offs3, offs4,
+    w1, w2_words, w2_scales, gain1, gain2, w3_words, w3_scales, w4, wg1, wg2, page1, out,
+):
+    nc = tc.nc
+    with ExitStack() as ctx:
+        lists = ctx.enter_context(tc.tile_pool(name="lists", bufs=1))
+        keep = ctx.enter_context(tc.tile_pool(name="keep", bufs=1))
+        ring = ctx.enter_context(tc.tile_pool(name="ring", bufs=2))
+        psum = ctx.enter_context(tc.psum_pool(name="psum", bufs=4))
+
+        def load_list(source, name):
+            tile = lists.tile(list(source.shape), U16, name=name)
+            nc.sync.dma_start(tile[:], source)
+            return tile
+
+        def load_words(source, name):
+            tile = keep.tile([P, T], U32, name=name, align_bytes=64)
+            nc.sync.dma_start(tile[:].bitcast(I32), source.rearrange("p t i -> p (t i)").bitcast(I32))
+            return tile
+
+        def load_weight(source):
+            tile = ring.tile([P, PACK, BANK], F32, name="raw", bufs=4)
+            nc.sync.dma_start(tile[:], source.rearrange("(p i) c -> p i c", i=PACK))
+            return tile
+
+        def load_plain(source, shape, name):
+            tile = keep.tile(shape, F32, name=name)
+            nc.sync.dma_start(tile[:], source)
+            return tile
+
+        def zeroed_plane(width, name):
+            tile = keep.tile([P, width], U8, name=name, align_bytes=64)
+            nc.vector.memset(tile[:].bitcast(I32), 0)
+            return tile
+
+        def quantise(grouped, name):
+            width = grouped.shape[1] // PACK
+            codes = keep.tile([P, width], U32, name=name + "_codes", align_bytes=64)
+            plane = keep.tile([P, width], U8, name=name + "_plane", align_bytes=64)
+            nc.vector.quantize_mx(codes[:].bitcast(FP8X4), plane[:], grouped[:])
+            return codes, plane
+
+        def gather_bytes(window, offsets, dtype, name):
+            tile = keep.tile([P, 16 * offsets.shape[1]], dtype, name=name, align_bytes=64)
+            nc.vector.tensor_copy(tile[:], window[:].indirect(offsets))
+            return tile
+
+        def load_plane(tile, rows, source):
+            for q in range(4):
+                nc.sync.dma_start(tile[32 * q : 32 * q + rows, :].bitcast(I32), source[:, 4 * q : 4 * q + 4, :].bitcast(I32))
+
+        tab_plane = zeroed_plane(T, "tab_plane")
+        w2_plane_raw = zeroed_plane(H, "w2_plane_raw")
+        tab2_plane = zeroed_plane(T, "tab2_plane")
+        w3_plane = zeroed_plane(2 * N, "w3_plane")
+
+        tab_tiles, w1_raw = {}, {}
+        doc_list = load_list(offs, "doc_list")
+        w1_raw[0, 0] = load_weight(w1[0:PASS, 0:PASS])
+        load_plane(tab_plane, 8, tab_scales)
+        tab_tiles[0] = load_words(tab_words[0], "tab0")
+        credit_list = load_list(offs2, "credit_list")
+        w1_raw[1, 0] = load_weight(w1[PASS : 2 * PASS, 0:PASS])
+        load_plane(tab2_plane, 4, tab2_scales)
+        w1_raw[0, 1] = load_weight(w1[0:PASS, PASS : 2 * PASS])
+        w2_raw = keep.tile([P, 2 * H], U8, name="w2_raw")
+        nc.sync.dma_start(w2_raw[:].bitcast(I32), w2_words[0].bitcast(I32))
+        tab_tiles[1] = load_words(tab_words[1], "tab1")
+        load_plane(w2_plane_raw, 4, w2_scales)
+        tab2_tile = load_words(tab2_words[0], "tab_credits")
+        pair_list = load_list(pos1, "pair_list")
+        g2 = load_plain(gain2.rearrange("(b p t) -> p b t", b=2, t=PACK), [P, 2, PACK], "g2")
+        w1_raw[1, 1] = load_weight(w1[PASS : 2 * PASS, PASS : 2 * PASS])
+        g1 = load_plain(gain1.rearrange("(b p t) -> p b t", b=2, t=PACK), [P, 2, PACK], "g1")
+        w3_codes = keep.tile([P, 2, 2 * N], U8, name="w3_codes", align_bytes=64)
+        nc.sync.dma_start(w3_codes[:].bitcast(I32), w3_words.bitcast(I32).rearrange("b p n -> p b n"))
+        doc_slots = load_list(offs3, "doc_slots")
+        wg1_tile = load_plain(wg1, [P, S], "wg1_tile")
+        for q in range(4):
+            nc.sync.dma_start(
+                w3_plane[32 * q : 32 * q + 4, :].bitcast(I32).rearrange("r (b n) -> r b n", b=2),
+                w3_scales[:, 4 * q : 4 * q + 4, :].bitcast(I32).rearrange("b r n -> r b n"),
+            )
+        pages = [load_plain(page1[P * n : P * (n + 1), :], [P, T2], "page%d" % n) for n in range(N // P)]
+        credit_slots = load_list(offs4, "credit_slots")
+        wg2_tile = load_plain(wg2, [P, C], "wg2_tile")
+
+        v_plane = gather_bytes(tab_plane, doc_list[:], U8, "v_plane")
+        v_words = {}
+
+        def gather_docs(a):
+            for half in range(S // BANK):
+                entries = doc_list[:, BANK // 16 * half : BANK // 16 * (half + 1)]
+                v_words[a, half] = gather_bytes(tab_tiles[a], entries, U32, "v_words%d%d" % (a, half))
+
+        gather_docs(0)
+
+        w1_q = {}
+
+        def quantise_w1(a, b, on_scalar):
+            grouped = ring.tile([P, PACK * BANK], BF16, name="grouped", bufs=3, align_bytes=64)
+            dealt = grouped[:].rearrange("p (t m i) -> p m i t", t=PACK, i=PACK)
+            rows = w1_raw[a, b][:].rearrange("p i (m t) -> p m i t", t=PACK)
+            if on_scalar > 0:
+                nc.scalar.copy(dealt[:, 0:on_scalar], rows[:, 0:on_scalar])
+            if on_scalar < P:
+                nc.vector.tensor_copy(dealt[:, on_scalar:P], rows[:, on_scalar:P])
+            w1_q[a, b] = quantise(grouped, "w1_%d%d" % (a, b))
+
+        h1 = {(b, t): keep.tile([P, S], F32, name="h1_%d%d" % (b, t)) for b in range(2) for t in range(PACK)}
+
+        def doc_features(b, t, halves=(0, 1)):
+            rows = slice(P * t, P * (t + 1))
+            for half in halves:
+                cols = slice(BANK * half, BANK * (half + 1))
+                bank = psum.tile([P, BANK], F32, name="h_bank")
+                for a in range(2):
+                    codes, plane = w1_q[a, b]
+                    nc.tensor.matmul_mx(
+                        bank[:], codes[:, rows].bitcast(FP8X4), plane[:, rows],
+                        v_words[a, half][:].bitcast(FP8X4), v_plane[4 * a : P, cols],
+                        start=(a == 0), stop=(a == 1),
+                    )
+                nc.scalar.copy(h1[b, t][:, cols], bank[:])
+
+        quantise_w1(0, 0, P)
+        quantise_w1(1, 0, 128)
+        v2_plane = gather_bytes(tab2_plane, credit_list[:], U8, "v2_plane")
+        w2_codes = keep.tile([P, 2 * H], U8, name="w2_codes", align_bytes=64)
+        nc.vector.tensor_copy(
+            w2_codes[:].bitcast(U16).rearrange("p (b t m) -> p b t m", b=2, t=PACK),
+            w2_raw[:].bitcast(U16).rearrange("p (b m t) -> p b t m", b=2, t=PACK),
+        )
+        gather_docs(1)
+        v2_words = gather_bytes(tab2_tile, credit_list[:], U32, "v2_words")
+        w2_plane = keep.tile([P, H], U8, name="w2_plane", align_bytes=64)
+        nc.vector.tensor_copy(
+            w2_plane[:].rearrange("p (b t m) -> p b t m", b=2, t=PACK),
+            w2_plane_raw[:].rearrange("p (b m t) -> p b t m", b=2, t=PACK),
+        )
+
+        def interleave(slots, width):
+            grouped = ring.tile([P, PACK * width], BF16, name="grouped", bufs=3, align_bytes=64)
+            nc.scalar.copy(
+                grouped[:].rearrange("p (c i t) -> p c t i", i=4, t=PACK),
+                slots[:].rearrange("p t (c i) -> p c t i", i=4),
+            )
+            return grouped
+
+        z2_slots = [keep.tile([P, PACK, C], BF16, name="z2_slots%d" % b) for b in range(2)]
+
+        h2 = {}
+
+        def credit_features(b, t):
+            col = PASS * b + P * t
+            bank = psum.tile([P, BANK], F32, name="h_bank")
+            nc.tensor.matmul_mx(
+                bank[:], w2_codes[:, 2 * col : 2 * (col + P)].bitcast(FP4X4), w2_plane[:, col : col + P],
+                v2_words[:].bitcast(FP8X4), v2_plane[:], start=True, stop=True,
+            )
+            h2[b, t] = ring.tile([P, C], F32, name="h2", bufs=5)
+            nc.scalar.copy(h2[b, t][:], bank[:])
+
+        total = {}
+
+        def pair_sum(b, t):
+            total[b, t] = ring.tile([P, C], F32, name="total", bufs=2)
+            nc.vector.tensor_tensor(total[b, t][:], h1[b, t][:].indirect(pair_list[:]), h2[b, t][:], ADD)
+
+        def pair_product(b, t):
+            nc.vector.scalar_tensor_tensor(z2_slots[b][:, t, :], total[b, t][:], g2[:, b, t : t + 1], h2[b, t][:], MULT, MULT)
+
+        z1_q = {}
+
+        def square_docs(c, b, on_vector=False):
+            cols = slice(CHUNK * c, CHUNK * (c + 1))
+            slots = ring.tile([P, PACK, CHUNK], BF16, name="z1_slots", bufs=2)
+            if on_vector:
+                for t in range(PACK):
+                    nc.vector.scalar_tensor_tensor(slots[:, t, :], h1[b, t][:, cols], g1[:, b, t : t + 1], h1[b, t][:, cols], MULT, MULT)
+            else:
+                squares = ring.tile([P, PACK, CHUNK], F32, name="squares", bufs=1)
+                for t in range(PACK):
+                    nc.scalar.activation(squares[:, t, :], h1[b, t][:, cols], SQUARE)
+                for t in range(PACK):
+                    nc.scalar.activation(slots[:, t, :], squares[:, t, :], COPY, scale=g1[:, b, t : t + 1])
+            z1_q[c, b] = quantise(interleave(slots, CHUNK), "z1_%d%d" % (c, b))
+
+        y_banks = {}
+
+        def score_docs(parts):
+            bank = psum.tile([P, 2 * CHUNK], F32, name="y_bank")
+            for i, (c, n) in enumerate(parts):
+                for b in range(2):
+                    codes, plane = z1_q[c, b]
+                    nc.tensor.matmul_mx(
+                        bank[:, CHUNK * i : CHUNK * (i + 1)], w3_codes[:, b, 2 * P * n : 2 * P * (n + 1)].bitcast(FP4X4),
+                        w3_plane[:, N * b + P * n : N * b + P * (n + 1)],
+                        codes[:].bitcast(FP8X4), plane[:], start=(b == 0), stop=(b == 1),
+                    )
+            y_banks[parts] = bank
+
+        def scatter_docs(n, values, first, width):
+            slots = doc_slots[:, first // 16 : (first + width) // 16]
+            nc.vector.tensor_tensor(pages[n][:].indirect(slots), values, wg1_tile[:, first : first + width], MULT)
+
+        def place_docs(parts):
+            staged = ring.tile([P, 2 * CHUNK], F32, name="staged", bufs=4)
+            nc.scalar.copy(staged[:], y_banks[parts][:])
+            if parts[0][1] == parts[1][1]:
+                scatter_docs(parts[0][1], staged[:], CHUNK * parts[0][0], 2 * CHUNK)
+            else:
+                for i, (c, n) in enumerate(parts):
+                    scatter_docs(n, staged[:, CHUNK * i : CHUNK * (i + 1)], CHUNK * c, CHUNK)
+
+        w4_q, z2_q = {}, {}
+
+        def quantise_w4(b, copy):
+            raw = load_weight(w4[PASS * b : PASS * (b + 1), :])
+            grouped = ring.tile([P, PACK * N], BF16, name="grouped", bufs=3, align_bytes=64)
+            copy(
+                grouped[:].rearrange("p (c i t) -> p c t i", i=4, t=PACK),
+                raw[:].rearrange("p t (c i) -> p c t i", i=4),
+            )
+            w4_q[b] = quantise(grouped, "w4_%d" % b)
+
+        def quantise_z2(b):
+            z2_q[b] = quantise(interleave(z2_slots[b], C), "z2_%d" % b)
+
+        def score_credits():
+            for n in range(N // P):
+                rows = slice(P * n, P * (n + 1))
+                bank = psum.tile([P, C], F32, name="y_bank")
+                for b in range(2):
+                    nc.tensor.matmul_mx(
+                        bank[:], w4_q[b][0][:, rows].bitcast(FP8X4), w4_q[b][1][:, rows],
+                        z2_q[b][0][:].bitcast(FP8X4), z2_q[b][1][:], start=(b == 0), stop=(b == 1),
+                    )
+                y_banks["credits", n] = bank
+
+        def place_credits(n):
+            staged = ring.tile([P, C], F32, name="staged", bufs=4)
+            nc.scalar.copy(staged[:], y_banks["credits", n][:])
+            nc.vector.tensor_tensor(pages[n][:].indirect(credit_slots[:]), staged[:], wg2_tile[:], MULT)
+
+        def store(n):
+            nc.sync.dma_start(out[P * n : P * (n + 1), :], pages[n][:])
+
+        quantise_w1(0, 1, 128)
+        quantise_w1(1, 1, 0)
+        doc_features(0, 0, (0,))
+        doc_features(0, 1, (0,))
+        doc_features(0, 2, (0,))
+        doc_features(0, 3, (0,))
+        doc_features(0, 0, (1,))
+        doc_features(0, 1, (1,))
+        doc_features(0, 2, (1,))
+        doc_features(0, 3, (1,))
+        credit_features(0, 0)
+        credit_features(0, 1)
+        doc_features(1, 0)
+        credit_features(0, 2)
+        doc_features(1, 1)
+        credit_features(0, 3)
+        doc_features(1, 2)
+        doc_features(1, 3)
+        pair_sum(0, 0)
+        pair_sum(0, 1)
+        pair_product(0, 0)
+        pair_sum(0, 2)
+        pair_product(0, 1)
+        pair_sum(0, 3)
+        pair_product(0, 2)
+        pair_product(0, 3)
+        credit_features(1, 0)
+        credit_features(1, 1)
+        square_docs(0, 0)
+        credit_features(1, 2)
+        pair_sum(1, 0)
+        pair_sum(1, 1)
+        pair_product(1, 0)
+        pair_sum(1, 2)
+        pair_product(1, 1)
+        pair_product(1, 2)
+        square_docs(0, 1)
+        credit_features(1, 3)
+        score_docs(((0, 0), (0, 1)))
+        score_docs(((0, 2), (0, 3)))
+        pair_sum(1, 3)
+        pair_product(1, 3)
+        square_docs(1, 0)
+        place_docs(((0, 0), (0, 1)))
+        square_docs(1, 1, True)
+        place_docs(((0, 2), (0, 3)))
+        score_docs(((1, 0), (1, 1)))
+        score_docs(((1, 2), (1, 3)))
+        quantise_w4(0, nc.scalar.copy)
+        quantise_z2(0)
+        place_docs(((1, 0), (1, 1)))
+        quantise_w4(1, nc.vector.tensor_copy)
+        quantise_z2(1)
+        place_docs(((1, 2), (1, 3)))
+        score_credits()
+        square_docs(2, 0)
+        place_credits(0)
+        place_credits(1)
+        square_docs(2, 1)
+        score_docs(((2, 0), (2, 1)))
+        square_docs(3, 0)
+        place_credits(2)
+        square_docs(3, 1)
+        place_credits(3)
+        place_docs(((2, 0), (2, 1)))
+        score_docs(((3, 0), (3, 1)))
+        score_docs(((2, 2), (3, 2)))
+        score_docs(((2, 3), (3, 3)))
+        place_docs(((3, 0), (3, 1)))
+        store(0)
+        store(1)
+        place_docs(((2, 2), (3, 2)))
+        store(2)
+        place_docs(((2, 3), (3, 3)))
+        store(3)

@@ -23,6 +23,9 @@ PACK = 4
 PASS = P * PACK
 BANK = 512
 CHUNK = 256
+PER_COLUMN = 16
+RUN = 4
+QUADRANTS = 4
 
 
 def tile_list_credit_discrepancy_page_kernel(
@@ -33,8 +36,28 @@ def tile_list_credit_discrepancy_page_kernel(
     with ExitStack() as ctx:
         lists = ctx.enter_context(tc.tile_pool(name="lists", bufs=1))
         keep = ctx.enter_context(tc.tile_pool(name="keep", bufs=1))
-        ring = ctx.enter_context(tc.tile_pool(name="ring", bufs=2))
-        psum = ctx.enter_context(tc.psum_pool(name="psum", bufs=4))
+        psum = ctx.enter_context(tc.psum_pool(name="psum", bufs=1))
+
+        def rotation(tiles):
+            def take():
+                tiles.append(tiles.pop(0))
+                return tiles[-1]
+
+            return take
+
+        def buffers(count, shape, dtype, name):
+            return rotation([keep.tile(shape, dtype, name="%s%d" % (name, i), align_bytes=64) for i in range(count)])
+
+        take_raw = buffers(4, [P, PACK, BANK], F32, "raw")
+        take_woven = buffers(3, [P, PACK * BANK], BF16, "woven")
+        take_z1_woven = buffers(4, [P, PACK * CHUNK], BF16, "z1_woven")
+        take_h2 = buffers(PACK, [P, C], F32, "h2_")
+        take_z1_rows = buffers(4, [P, PACK, CHUNK], BF16, "z1_rows")
+        take_staged = buffers(2, [P, BANK], F32, "staged")
+        take_h_bank = rotation([psum.tile([P, BANK], F32, name="h_bank%d" % i) for i in range(4)])
+        take_y_bank = rotation([psum.tile([P, BANK], F32, name="y_bank%d" % i) for i in range(4)])
+        squares = keep.tile([P, PACK, CHUNK], F32, name="squares")
+        woven_then_sums = keep.tile([P, PACK * BANK], BF16, name="woven_then_sums", align_bytes=64)
 
         def load_list(source, name):
             tile = lists.tile(list(source.shape), U16, name=name)
@@ -47,7 +70,7 @@ def tile_list_credit_discrepancy_page_kernel(
             return tile
 
         def load_weight(source):
-            tile = ring.tile([P, PACK, BANK], F32, name="raw", bufs=4)
+            tile = take_raw()
             nc.sync.dma_start(tile[:], source.rearrange("(p i) c -> p i c", i=PACK))
             return tile
 
@@ -56,26 +79,43 @@ def tile_list_credit_discrepancy_page_kernel(
             nc.sync.dma_start(tile[:], source)
             return tile
 
+        def load_gain(source, name):
+            return load_plain(source.rearrange("(b p t) -> p b t", b=2, t=PACK), [P, 2, PACK], name)
+
+        def load_page(n):
+            return load_plain(page1[P * n : P * (n + 1), :], [P, T2], "page%d" % n)
+
         def zeroed_plane(width, name):
             tile = keep.tile([P, width], U8, name=name, align_bytes=64)
             nc.vector.memset(tile[:].bitcast(I32), 0)
             return tile
 
-        def quantise(grouped, name):
-            width = grouped.shape[1] // PACK
+        def load_plane(tile, source):
+            rows = 4 * source.shape[0]
+            for q in range(QUADRANTS):
+                nc.sync.dma_start(tile[32 * q : 32 * q + rows, :].bitcast(I32), source[:, 4 * q : 4 * q + 4, :].bitcast(I32))
+
+        def quantise(woven, name):
+            width = woven.shape[1] // PACK
             codes = keep.tile([P, width], U32, name=name + "_codes", align_bytes=64)
             plane = keep.tile([P, width], U8, name=name + "_plane", align_bytes=64)
-            nc.vector.quantize_mx(codes[:].bitcast(FP8X4), plane[:], grouped[:])
+            nc.vector.quantize_mx(codes[:].bitcast(FP8X4), plane[:], woven[:])
             return codes, plane
 
         def gather_bytes(window, offsets, dtype, name):
-            tile = keep.tile([P, 16 * offsets.shape[1]], dtype, name=name, align_bytes=64)
+            tile = keep.tile([P, PER_COLUMN * offsets.shape[1]], dtype, name=name, align_bytes=64)
             nc.vector.tensor_copy(tile[:], window[:].indirect(offsets))
             return tile
 
-        def load_plane(tile, rows, source):
-            for q in range(4):
-                nc.sync.dma_start(tile[32 * q : 32 * q + rows, :].bitcast(I32), source[:, 4 * q : 4 * q + 4, :].bitcast(I32))
+        def entries(list_tile, first, count):
+            return list_tile[:, first // PER_COLUMN : (first + count) // PER_COLUMN]
+
+        def weave(rows, woven):
+            nc.scalar.copy(
+                woven[:].rearrange("p (c i t) -> p c t i", i=RUN, t=PACK),
+                rows[:].rearrange("p t (c i) -> p c t i", i=RUN),
+            )
+            return woven
 
         tab_plane = zeroed_plane(T, "tab_plane")
         w2_plane_raw = zeroed_plane(H, "w2_plane_raw")
@@ -85,139 +125,138 @@ def tile_list_credit_discrepancy_page_kernel(
         tab_tiles, w1_raw = {}, {}
         doc_list = load_list(offs, "doc_list")
         w1_raw[0, 0] = load_weight(w1[0:PASS, 0:PASS])
-        load_plane(tab_plane, 8, tab_scales)
-        tab_tiles[0] = load_words(tab_words[0], "tab0")
+        load_plane(tab_plane, tab_scales)
+        tab_tiles[0] = load_words(tab_words[0], "tab_pass0")
         credit_list = load_list(offs2, "credit_list")
-        w1_raw[1, 0] = load_weight(w1[PASS : 2 * PASS, 0:PASS])
-        load_plane(tab2_plane, 4, tab2_scales)
-        w1_raw[0, 1] = load_weight(w1[0:PASS, PASS : 2 * PASS])
+        load_plane(tab2_plane, tab2_scales)
+        w1_raw[1, 0] = load_weight(w1[PASS:K, 0:PASS])
         w2_raw = keep.tile([P, 2 * H], U8, name="w2_raw")
         nc.sync.dma_start(w2_raw[:].bitcast(I32), w2_words[0].bitcast(I32))
-        tab_tiles[1] = load_words(tab_words[1], "tab1")
-        load_plane(w2_plane_raw, 4, w2_scales)
-        tab2_tile = load_words(tab2_words[0], "tab_credits")
+        load_plane(w2_plane_raw, w2_scales)
+        tab_tiles[1] = load_words(tab_words[1], "tab_pass1")
+        tab2_tile = load_words(tab2_words[0], "tab2_pass0")
+        w1_raw[0, 1] = load_weight(w1[0:PASS, PASS:H])
         pair_list = load_list(pos1, "pair_list")
-        g2 = load_plain(gain2.rearrange("(b p t) -> p b t", b=2, t=PACK), [P, 2, PACK], "g2")
-        w1_raw[1, 1] = load_weight(w1[PASS : 2 * PASS, PASS : 2 * PASS])
-        g1 = load_plain(gain1.rearrange("(b p t) -> p b t", b=2, t=PACK), [P, 2, PACK], "g1")
+        g2 = load_gain(gain2, "g2")
+        w1_raw[1, 1] = load_weight(w1[PASS:K, PASS:H])
+
+        v_words, w1_q = {}, {}
+
+        def gather_docs(a):
+            for half in range(S // BANK):
+                offsets = entries(doc_list, BANK * half, BANK)
+                v_words[a, half] = gather_bytes(tab_tiles[a], offsets, U32, "v_words%d%d" % (a, half))
+
+        def quantise_w1(a, b, copy, woven):
+            copy(
+                woven[:].rearrange("p (t m i) -> p m i t", t=PACK, i=PACK),
+                w1_raw[a, b][:].rearrange("p i (m t) -> p m i t", t=PACK),
+            )
+            w1_q[a, b] = quantise(woven, "w1_%d%d" % (a, b))
+
+        v_plane = gather_bytes(tab_plane, doc_list[:], U8, "v_plane")
+        gather_docs(0)
+        quantise_w1(0, 0, nc.scalar.copy, take_woven())
+        quantise_w1(1, 0, nc.scalar.copy, take_woven())
+
+        g1 = load_gain(gain1, "g1")
         w3_codes = keep.tile([P, 2, 2 * N], U8, name="w3_codes", align_bytes=64)
         nc.sync.dma_start(w3_codes[:].bitcast(I32), w3_words.bitcast(I32).rearrange("b p n -> p b n"))
-        doc_slots = load_list(offs3, "doc_slots")
-        wg1_tile = load_plain(wg1, [P, S], "wg1_tile")
-        for q in range(4):
+        for q in range(QUADRANTS):
             nc.sync.dma_start(
                 w3_plane[32 * q : 32 * q + 4, :].bitcast(I32).rearrange("r (b n) -> r b n", b=2),
                 w3_scales[:, 4 * q : 4 * q + 4, :].bitcast(I32).rearrange("b r n -> r b n"),
             )
-        pages = [load_plain(page1[P * n : P * (n + 1), :], [P, T2], "page%d" % n) for n in range(N // P)]
+        doc_slots = load_list(offs3, "doc_slots")
+        wg1_tile = load_plain(wg1, [P, S], "wg1_tile")
+        pages = [load_page(0), load_page(1)]
+        w4_raw = [load_weight(w4[PASS * b : PASS * (b + 1), :]) for b in range(2)]
+        pages.extend([load_page(2), load_page(3)])
         credit_slots = load_list(offs4, "credit_slots")
         wg2_tile = load_plain(wg2, [P, C], "wg2_tile")
 
-        v_plane = gather_bytes(tab_plane, doc_list[:], U8, "v_plane")
-        v_words = {}
-
-        def gather_docs(a):
-            for half in range(S // BANK):
-                entries = doc_list[:, BANK // 16 * half : BANK // 16 * (half + 1)]
-                v_words[a, half] = gather_bytes(tab_tiles[a], entries, U32, "v_words%d%d" % (a, half))
-
-        gather_docs(0)
-
-        w1_q = {}
-
-        def quantise_w1(a, b, on_scalar):
-            grouped = ring.tile([P, PACK * BANK], BF16, name="grouped", bufs=3, align_bytes=64)
-            dealt = grouped[:].rearrange("p (t m i) -> p m i t", t=PACK, i=PACK)
-            rows = w1_raw[a, b][:].rearrange("p i (m t) -> p m i t", t=PACK)
-            if on_scalar > 0:
-                nc.scalar.copy(dealt[:, 0:on_scalar], rows[:, 0:on_scalar])
-            if on_scalar < P:
-                nc.vector.tensor_copy(dealt[:, on_scalar:P], rows[:, on_scalar:P])
-            w1_q[a, b] = quantise(grouped, "w1_%d%d" % (a, b))
+        v2_plane = gather_bytes(tab2_plane, credit_list[:], U8, "v2_plane")
+        gather_docs(1)
+        w2_codes = keep.tile([P, 2 * H], U8, name="w2_codes", align_bytes=64)
+        w2_plane = keep.tile([P, H], U8, name="w2_plane", align_bytes=64)
+        for b in range(2):
+            nc.gpsimd.tensor_copy(
+                w2_codes[:].rearrange("p (b t m e) -> p b t m e", b=2, t=PACK, e=2)[:, b],
+                w2_raw[:].rearrange("p (b m t e) -> p b t m e", b=2, t=PACK, e=2)[:, b],
+            )
+            nc.gpsimd.tensor_copy(
+                w2_plane[:].rearrange("p (b t m) -> p b t m", b=2, t=PACK)[:, b],
+                w2_plane_raw[:].rearrange("p (b m t) -> p b t m", b=2, t=PACK)[:, b],
+            )
+        v2_words = gather_bytes(tab2_tile, credit_list[:], U32, "v2_words")
 
         h1 = {(b, t): keep.tile([P, S], F32, name="h1_%d%d" % (b, t)) for b in range(2) for t in range(PACK)}
+        z2_rows = [keep.tile([P, PACK, C], BF16, name="z2_rows%d" % b) for b in range(2)]
+        h2, z1_q, w4_q, z2_q, spent, y_banks = {}, {}, {}, {}, {}, {}
 
-        def doc_features(b, t, halves=(0, 1)):
+        def doc_features(b, t, half):
             rows = slice(P * t, P * (t + 1))
-            for half in halves:
-                cols = slice(BANK * half, BANK * (half + 1))
-                bank = psum.tile([P, BANK], F32, name="h_bank")
-                for a in range(2):
-                    codes, plane = w1_q[a, b]
-                    nc.tensor.matmul_mx(
-                        bank[:], codes[:, rows].bitcast(FP8X4), plane[:, rows],
-                        v_words[a, half][:].bitcast(FP8X4), v_plane[4 * a : P, cols],
-                        start=(a == 0), stop=(a == 1),
-                    )
-                nc.scalar.copy(h1[b, t][:, cols], bank[:])
-
-        quantise_w1(0, 0, P)
-        quantise_w1(1, 0, 128)
-        v2_plane = gather_bytes(tab2_plane, credit_list[:], U8, "v2_plane")
-        w2_codes = keep.tile([P, 2 * H], U8, name="w2_codes", align_bytes=64)
-        nc.vector.tensor_copy(
-            w2_codes[:].bitcast(U16).rearrange("p (b t m) -> p b t m", b=2, t=PACK),
-            w2_raw[:].bitcast(U16).rearrange("p (b m t) -> p b t m", b=2, t=PACK),
-        )
-        gather_docs(1)
-        v2_words = gather_bytes(tab2_tile, credit_list[:], U32, "v2_words")
-        w2_plane = keep.tile([P, H], U8, name="w2_plane", align_bytes=64)
-        nc.vector.tensor_copy(
-            w2_plane[:].rearrange("p (b t m) -> p b t m", b=2, t=PACK),
-            w2_plane_raw[:].rearrange("p (b m t) -> p b t m", b=2, t=PACK),
-        )
-
-        def interleave(slots, width):
-            grouped = ring.tile([P, PACK * width], BF16, name="grouped", bufs=3, align_bytes=64)
-            nc.scalar.copy(
-                grouped[:].rearrange("p (c i t) -> p c t i", i=4, t=PACK),
-                slots[:].rearrange("p t (c i) -> p c t i", i=4),
-            )
-            return grouped
-
-        z2_slots = [keep.tile([P, PACK, C], BF16, name="z2_slots%d" % b) for b in range(2)]
-
-        h2 = {}
+            cols = slice(BANK * half, BANK * (half + 1))
+            bank = take_h_bank()
+            for a in range(2):
+                codes, plane = w1_q[a, b]
+                nc.tensor.matmul_mx(
+                    bank[:], codes[:, rows].bitcast(FP8X4), plane[:, rows],
+                    v_words[a, half][:].bitcast(FP8X4), v_plane[4 * a : P, cols],
+                    start=(a == 0), stop=(a == 1),
+                )
+            nc.scalar.copy(h1[b, t][:, cols], bank[:])
 
         def credit_features(b, t):
             col = PASS * b + P * t
-            bank = psum.tile([P, BANK], F32, name="h_bank")
+            bank = take_h_bank()
             nc.tensor.matmul_mx(
                 bank[:], w2_codes[:, 2 * col : 2 * (col + P)].bitcast(FP4X4), w2_plane[:, col : col + P],
                 v2_words[:].bitcast(FP8X4), v2_plane[:], start=True, stop=True,
             )
-            h2[b, t] = ring.tile([P, C], F32, name="h2", bufs=5)
+            h2[b, t] = take_h2()
             nc.scalar.copy(h2[b, t][:], bank[:])
 
-        total = {}
+        def pair_credits(b):
+            sums = woven_then_sums[:].bitcast(F32).rearrange("p (side c) -> p side c", side=2)
+            for step in range(PACK + 1):
+                if step < PACK:
+                    nc.vector.tensor_tensor(sums[:, step % 2, :], h1[b, step][:].indirect(pair_list[:]), h2[b, step][:], ADD)
+                if step > 0:
+                    t = step - 1
+                    nc.vector.scalar_tensor_tensor(z2_rows[b][:, t, :], sums[:, t % 2, :], g2[:, b, t : t + 1], h2[b, t][:], MULT, MULT)
 
-        def pair_sum(b, t):
-            total[b, t] = ring.tile([P, C], F32, name="total", bufs=2)
-            nc.vector.tensor_tensor(total[b, t][:], h1[b, t][:].indirect(pair_list[:]), h2[b, t][:], ADD)
+        def square_on_scalar(rows, b, cols):
+            for t in range(PACK):
+                nc.scalar.activation(squares[:, t, :], h1[b, t][:, cols], SQUARE)
+            for t in range(PACK):
+                nc.scalar.activation(rows[:, t, :], squares[:, t, :], COPY, scale=g1[:, b, t : t + 1])
 
-        def pair_product(b, t):
-            nc.vector.scalar_tensor_tensor(z2_slots[b][:, t, :], total[b, t][:], g2[:, b, t : t + 1], h2[b, t][:], MULT, MULT)
+        def square_on_vector(rows, b, cols):
+            for t in range(PACK):
+                values = h1[b, t][:, cols]
+                nc.vector.scalar_tensor_tensor(rows[:, t, :], values, g1[:, b, t : t + 1], values, MULT, MULT)
 
-        z1_q = {}
+        def quantise_z1(c, b, square=square_on_scalar):
+            rows = take_z1_rows()
+            square(rows, b, slice(CHUNK * c, CHUNK * (c + 1)))
+            z1_q[c, b] = quantise(weave(rows, take_z1_woven()), "z1_%d%d" % (c, b))
+            spent[c, b] = rows[:].rearrange("p t c -> p (t c)").bitcast(F32)
 
-        def square_docs(c, b, on_vector=False):
-            cols = slice(CHUNK * c, CHUNK * (c + 1))
-            slots = ring.tile([P, PACK, CHUNK], BF16, name="z1_slots", bufs=2)
-            if on_vector:
-                for t in range(PACK):
-                    nc.vector.scalar_tensor_tensor(slots[:, t, :], h1[b, t][:, cols], g1[:, b, t : t + 1], h1[b, t][:, cols], MULT, MULT)
-            else:
-                squares = ring.tile([P, PACK, CHUNK], F32, name="squares", bufs=1)
-                for t in range(PACK):
-                    nc.scalar.activation(squares[:, t, :], h1[b, t][:, cols], SQUARE)
-                for t in range(PACK):
-                    nc.scalar.activation(slots[:, t, :], squares[:, t, :], COPY, scale=g1[:, b, t : t + 1])
-            z1_q[c, b] = quantise(interleave(slots, CHUNK), "z1_%d%d" % (c, b))
+        def quantise_w4(b):
+            w4_q[b] = quantise(weave(w4_raw[b], take_woven()), "w4_%d" % b)
 
-        y_banks = {}
+        def quantise_z2(b):
+            z2_q[b] = quantise(weave(z2_rows[b], take_woven()), "z2_%d" % b)
+
+        def two_pages(c, pair):
+            return ((c, 2 * pair), (c, 2 * pair + 1))
+
+        def two_chunks(c, n):
+            return ((c, n), (c + 1, n))
 
         def score_docs(parts):
-            bank = psum.tile([P, 2 * CHUNK], F32, name="y_bank")
+            bank = take_y_bank()
             for i, (c, n) in enumerate(parts):
                 for b in range(2):
                     codes, plane = z1_q[c, b]
@@ -228,37 +267,10 @@ def tile_list_credit_discrepancy_page_kernel(
                     )
             y_banks[parts] = bank
 
-        def scatter_docs(n, values, first, width):
-            slots = doc_slots[:, first // 16 : (first + width) // 16]
-            nc.vector.tensor_tensor(pages[n][:].indirect(slots), values, wg1_tile[:, first : first + width], MULT)
-
-        def place_docs(parts):
-            staged = ring.tile([P, 2 * CHUNK], F32, name="staged", bufs=4)
-            nc.scalar.copy(staged[:], y_banks[parts][:])
-            if parts[0][1] == parts[1][1]:
-                scatter_docs(parts[0][1], staged[:], CHUNK * parts[0][0], 2 * CHUNK)
-            else:
-                for i, (c, n) in enumerate(parts):
-                    scatter_docs(n, staged[:, CHUNK * i : CHUNK * (i + 1)], CHUNK * c, CHUNK)
-
-        w4_q, z2_q = {}, {}
-
-        def quantise_w4(b, copy):
-            raw = load_weight(w4[PASS * b : PASS * (b + 1), :])
-            grouped = ring.tile([P, PACK * N], BF16, name="grouped", bufs=3, align_bytes=64)
-            copy(
-                grouped[:].rearrange("p (c i t) -> p c t i", i=4, t=PACK),
-                raw[:].rearrange("p t (c i) -> p c t i", i=4),
-            )
-            w4_q[b] = quantise(grouped, "w4_%d" % b)
-
-        def quantise_z2(b):
-            z2_q[b] = quantise(interleave(z2_slots[b], C), "z2_%d" % b)
-
         def score_credits():
             for n in range(N // P):
                 rows = slice(P * n, P * (n + 1))
-                bank = psum.tile([P, C], F32, name="y_bank")
+                bank = take_y_bank()
                 for b in range(2):
                     nc.tensor.matmul_mx(
                         bank[:], w4_q[b][0][:, rows].bitcast(FP8X4), w4_q[b][1][:, rows],
@@ -266,86 +278,82 @@ def tile_list_credit_discrepancy_page_kernel(
                     )
                 y_banks["credits", n] = bank
 
-        def place_credits(n):
-            staged = ring.tile([P, C], F32, name="staged", bufs=4)
-            nc.scalar.copy(staged[:], y_banks["credits", n][:])
+        def stage(bank, staged):
+            nc.scalar.copy(staged[:], bank[:])
+            return staged
+
+        def scatter_docs(n, values, first, count):
+            window = pages[n][:].indirect(entries(doc_slots, first, count))
+            nc.vector.tensor_tensor(window, values, wg1_tile[:, first : first + count], MULT)
+
+        def place_two_pages(c, pair, staged):
+            parts = two_pages(c, pair)
+            stage(y_banks[parts], staged)
+            for i, (chunk, n) in enumerate(parts):
+                scatter_docs(n, staged[:, CHUNK * i : CHUNK * (i + 1)], CHUNK * chunk, CHUNK)
+
+        def place_two_chunks(c, n):
+            staged = stage(y_banks[two_chunks(c, n)], take_staged())
+            scatter_docs(n, staged[:], CHUNK * c, 2 * CHUNK)
+
+        def place_credits(n, staged):
+            stage(y_banks["credits", n], staged)
             nc.vector.tensor_tensor(pages[n][:].indirect(credit_slots[:]), staged[:], wg2_tile[:], MULT)
 
         def store(n):
             nc.sync.dma_start(out[P * n : P * (n + 1), :], pages[n][:])
 
-        quantise_w1(0, 1, 128)
-        quantise_w1(1, 1, 0)
-        doc_features(0, 0, (0,))
-        doc_features(0, 1, (0,))
-        doc_features(0, 2, (0,))
-        doc_features(0, 3, (0,))
-        doc_features(0, 0, (1,))
-        doc_features(0, 1, (1,))
-        doc_features(0, 2, (1,))
-        doc_features(0, 3, (1,))
-        credit_features(0, 0)
-        credit_features(0, 1)
-        doc_features(1, 0)
-        credit_features(0, 2)
-        doc_features(1, 1)
-        credit_features(0, 3)
-        doc_features(1, 2)
-        doc_features(1, 3)
-        pair_sum(0, 0)
-        pair_sum(0, 1)
-        pair_product(0, 0)
-        pair_sum(0, 2)
-        pair_product(0, 1)
-        pair_sum(0, 3)
-        pair_product(0, 2)
-        pair_product(0, 3)
-        credit_features(1, 0)
-        credit_features(1, 1)
-        square_docs(0, 0)
-        credit_features(1, 2)
-        pair_sum(1, 0)
-        pair_sum(1, 1)
-        pair_product(1, 0)
-        pair_sum(1, 2)
-        pair_product(1, 1)
-        pair_product(1, 2)
-        square_docs(0, 1)
-        credit_features(1, 3)
-        score_docs(((0, 0), (0, 1)))
-        score_docs(((0, 2), (0, 3)))
-        pair_sum(1, 3)
-        pair_product(1, 3)
-        square_docs(1, 0)
-        place_docs(((0, 0), (0, 1)))
-        square_docs(1, 1, True)
-        place_docs(((0, 2), (0, 3)))
-        score_docs(((1, 0), (1, 1)))
-        score_docs(((1, 2), (1, 3)))
-        quantise_w4(0, nc.scalar.copy)
+        for half in range(S // BANK):
+            for t in range(PACK):
+                doc_features(0, t, half)
+        for t in range(PACK):
+            credit_features(0, t)
+        quantise_w1(0, 1, nc.vector.tensor_copy, take_woven())
+        quantise_w1(1, 1, nc.vector.tensor_copy, woven_then_sums)
+        pair_credits(0)
+        quantise_z1(0, 0, square_on_vector)
+
+        for t in range(PACK):
+            doc_features(1, t, 0)
+        quantise_z1(0, 1, square_on_vector)
+        for pair in range(2):
+            score_docs(two_pages(0, pair))
+        for t in range(PACK):
+            doc_features(1, t, 1)
+            credit_features(1, t)
         quantise_z2(0)
-        place_docs(((1, 0), (1, 1)))
-        quantise_w4(1, nc.vector.tensor_copy)
+        pair_credits(1)
+
+        place_two_pages(0, 0, take_staged())
+        for b in range(2):
+            quantise_z1(1, b)
+        place_two_pages(0, 1, take_staged())
+        for pair in range(2):
+            score_docs(two_pages(1, pair))
+        quantise_w4(0)
+        place_two_pages(1, 0, take_staged())
+        quantise_w4(1)
         quantise_z2(1)
-        place_docs(((1, 2), (1, 3)))
+        place_two_pages(1, 1, take_staged())
         score_credits()
-        square_docs(2, 0)
-        place_credits(0)
-        place_credits(1)
-        square_docs(2, 1)
-        score_docs(((2, 0), (2, 1)))
-        square_docs(3, 0)
-        place_credits(2)
-        square_docs(3, 1)
-        place_credits(3)
-        place_docs(((2, 0), (2, 1)))
-        score_docs(((3, 0), (3, 1)))
-        score_docs(((2, 2), (3, 2)))
-        score_docs(((2, 3), (3, 3)))
-        place_docs(((3, 0), (3, 1)))
+
+        quantise_z1(2, 0)
+        place_credits(0, take_staged())
+        place_credits(1, take_staged())
+        quantise_z1(2, 1)
+        score_docs(two_pages(2, 0))
+        place_credits(2, spent[2, 1])
+        quantise_z1(3, 0)
+        place_credits(3, spent[3, 0])
+        quantise_z1(3, 1)
+
+        place_two_pages(2, 0, spent[3, 1])
+        score_docs(two_pages(3, 0))
+        for n in (2, 3):
+            score_docs(two_chunks(2, n))
+        place_two_pages(3, 0, take_staged())
         store(0)
         store(1)
-        place_docs(((2, 2), (3, 2)))
-        store(2)
-        place_docs(((2, 3), (3, 3)))
-        store(3)
+        for n in (2, 3):
+            place_two_chunks(2, n)
+            store(n)

from contextlib import ExitStack

import concourse.mybir as mybir

K, M, T, S, C, H, N, T2 = 1024, 512, 2048, 1024, 512, 1024, 512, 2048
FLOPS = 2 * (K * H * S + M * H * C + H * N * S + H * N * C)

F32 = mybir.dt.float32
BF16 = mybir.dt.bfloat16
I32 = mybir.dt.int32
U32 = mybir.dt.uint32
U16 = mybir.dt.uint16
U8 = mybir.dt.uint8
FP8X4 = mybir.dt.float8_e4m3fn_x4
FP4X4 = mybir.dt.float4_e2m1fn_x4
MULT = mybir.AluOpType.mult
ADD = mybir.AluOpType.add
COPY = mybir.ActivationFunctionType.Copy
SQUARE = mybir.ActivationFunctionType.Square

P = 128
PACK = 4
PASS = P * PACK
BANK = 512
CHUNK = 256
PER_COLUMN = 16
RUN = 4
QUADRANTS = 4


def tile_list_credit_discrepancy_page_kernel(
    tc, tab_words, tab_scales, tab2_words, tab2_scales, offs, offs2, pos1, offs3, offs4,
    w1, w2_words, w2_scales, gain1, gain2, w3_words, w3_scales, w4, wg1, wg2, page1, out,
):
    nc = tc.nc
    with ExitStack() as ctx:
        lists = ctx.enter_context(tc.tile_pool(name="lists", bufs=1))
        keep = ctx.enter_context(tc.tile_pool(name="keep", bufs=1))
        psum = ctx.enter_context(tc.psum_pool(name="psum", bufs=1))

        def rotation(tiles):
            def take():
                tiles.append(tiles.pop(0))
                return tiles[-1]

            return take

        def buffers(count, shape, dtype, name):
            return rotation([keep.tile(shape, dtype, name="%s%d" % (name, i), align_bytes=64) for i in range(count)])

        take_raw = buffers(4, [P, PACK, BANK], F32, "raw")
        take_woven = buffers(3, [P, PACK * BANK], BF16, "woven")
        take_z1_woven = buffers(4, [P, PACK * CHUNK], BF16, "z1_woven")
        take_h2 = buffers(PACK, [P, C], F32, "h2_")
        take_z1_rows = buffers(4, [P, PACK, CHUNK], BF16, "z1_rows")
        take_staged = buffers(2, [P, BANK], F32, "staged")
        take_h_bank = rotation([psum.tile([P, BANK], F32, name="h_bank%d" % i) for i in range(4)])
        take_y_bank = rotation([psum.tile([P, BANK], F32, name="y_bank%d" % i) for i in range(4)])
        squares = keep.tile([P, PACK, CHUNK], F32, name="squares")
        woven_then_sums = keep.tile([P, PACK * BANK], BF16, name="woven_then_sums", align_bytes=64)

        def load_list(source, name):
            tile = lists.tile(list(source.shape), U16, name=name)
            nc.sync.dma_start(tile[:], source)
            return tile

        def load_words(source, name):
            tile = keep.tile([P, T], U32, name=name, align_bytes=64)
            nc.sync.dma_start(tile[:].bitcast(I32), source.rearrange("p t i -> p (t i)").bitcast(I32))
            return tile

        def load_weight(source):
            tile = take_raw()
            nc.sync.dma_start(tile[:], source.rearrange("(p i) c -> p i c", i=PACK))
            return tile

        def load_plain(source, shape, name):
            tile = keep.tile(shape, F32, name=name)
            nc.sync.dma_start(tile[:], source)
            return tile

        def load_gain(source, name):
            return load_plain(source.rearrange("(b p t) -> p b t", b=2, t=PACK), [P, 2, PACK], name)

        def load_page(n):
            return load_plain(page1[P * n : P * (n + 1), :], [P, T2], "page%d" % n)

        def zeroed_plane(width, name):
            tile = keep.tile([P, width], U8, name=name, align_bytes=64)
            nc.vector.memset(tile[:].bitcast(I32), 0)
            return tile

        def load_plane(tile, source):
            rows = 4 * source.shape[0]
            for q in range(QUADRANTS):
                nc.sync.dma_start(tile[32 * q : 32 * q + rows, :].bitcast(I32), source[:, 4 * q : 4 * q + 4, :].bitcast(I32))

        def quantise(woven, name):
            width = woven.shape[1] // PACK
            codes = keep.tile([P, width], U32, name=name + "_codes", align_bytes=64)
            plane = keep.tile([P, width], U8, name=name + "_plane", align_bytes=64)
            nc.vector.quantize_mx(codes[:].bitcast(FP8X4), plane[:], woven[:])
            return codes, plane

        def gather_bytes(window, offsets, dtype, name):
            tile = keep.tile([P, PER_COLUMN * offsets.shape[1]], dtype, name=name, align_bytes=64)
            nc.vector.tensor_copy(tile[:], window[:].indirect(offsets))
            return tile

        def entries(list_tile, first, count):
            return list_tile[:, first // PER_COLUMN : (first + count) // PER_COLUMN]

        def weave(rows, woven):
            nc.scalar.copy(
                woven[:].rearrange("p (c i t) -> p c t i", i=RUN, t=PACK),
                rows[:].rearrange("p t (c i) -> p c t i", i=RUN),
            )
            return woven

        tab_plane = zeroed_plane(T, "tab_plane")
        w2_plane_raw = zeroed_plane(H, "w2_plane_raw")
        tab2_plane = zeroed_plane(T, "tab2_plane")
        w3_plane = zeroed_plane(2 * N, "w3_plane")

        tab_tiles, w1_raw = {}, {}
        doc_list = load_list(offs, "doc_list")
        w1_raw[0, 0] = load_weight(w1[0:PASS, 0:PASS])
        load_plane(tab_plane, tab_scales)
        tab_tiles[0] = load_words(tab_words[0], "tab_pass0")
        credit_list = load_list(offs2, "credit_list")
        load_plane(tab2_plane, tab2_scales)
        w1_raw[1, 0] = load_weight(w1[PASS:K, 0:PASS])
        w2_raw = keep.tile([P, 2 * H], U8, name="w2_raw")
        nc.sync.dma_start(w2_raw[:].bitcast(I32), w2_words[0].bitcast(I32))
        load_plane(w2_plane_raw, w2_scales)
        tab_tiles[1] = load_words(tab_words[1], "tab_pass1")
        tab2_tile = load_words(tab2_words[0], "tab2_pass0")
        w1_raw[0, 1] = load_weight(w1[0:PASS, PASS:H])
        pair_list = load_list(pos1, "pair_list")
        g2 = load_gain(gain2, "g2")
        w1_raw[1, 1] = load_weight(w1[PASS:K, PASS:H])

        v_words, w1_q = {}, {}

        def gather_docs(a):
            for half in range(S // BANK):
                offsets = entries(doc_list, BANK * half, BANK)
                v_words[a, half] = gather_bytes(tab_tiles[a], offsets, U32, "v_words%d%d" % (a, half))

        def quantise_w1(a, b, copy, woven):
            copy(
                woven[:].rearrange("p (t m i) -> p m i t", t=PACK, i=PACK),
                w1_raw[a, b][:].rearrange("p i (m t) -> p m i t", t=PACK),
            )
            w1_q[a, b] = quantise(woven, "w1_%d%d" % (a, b))

        v_plane = gather_bytes(tab_plane, doc_list[:], U8, "v_plane")
        gather_docs(0)
        quantise_w1(0, 0, nc.scalar.copy, take_woven())
        quantise_w1(1, 0, nc.scalar.copy, take_woven())

        g1 = load_gain(gain1, "g1")
        w3_codes = keep.tile([P, 2, 2 * N], U8, name="w3_codes", align_bytes=64)
        nc.sync.dma_start(w3_codes[:].bitcast(I32), w3_words.bitcast(I32).rearrange("b p n -> p b n"))
        for q in range(QUADRANTS):
            nc.sync.dma_start(
                w3_plane[32 * q : 32 * q + 4, :].bitcast(I32).rearrange("r (b n) -> r b n", b=2),
                w3_scales[:, 4 * q : 4 * q + 4, :].bitcast(I32).rearrange("b r n -> r b n"),
            )
        doc_slots = load_list(offs3, "doc_slots")
        wg1_tile = load_plain(wg1, [P, S], "wg1_tile")
        pages = [load_page(0), load_page(1)]
        w4_raw = [load_weight(w4[PASS * b : PASS * (b + 1), :]) for b in range(2)]
        pages.extend([load_page(2), load_page(3)])
        credit_slots = load_list(offs4, "credit_slots")
        wg2_tile = load_plain(wg2, [P, C], "wg2_tile")

        v2_plane = gather_bytes(tab2_plane, credit_list[:], U8, "v2_plane")
        gather_docs(1)
        w2_codes = keep.tile([P, 2 * H], U8, name="w2_codes", align_bytes=64)
        w2_plane = keep.tile([P, H], U8, name="w2_plane", align_bytes=64)
        for b in range(2):
            nc.gpsimd.tensor_copy(
                w2_codes[:].rearrange("p (b t m e) -> p b t m e", b=2, t=PACK, e=2)[:, b],
                w2_raw[:].rearrange("p (b m t e) -> p b t m e", b=2, t=PACK, e=2)[:, b],
            )
            nc.gpsimd.tensor_copy(
                w2_plane[:].rearrange("p (b t m) -> p b t m", b=2, t=PACK)[:, b],
                w2_plane_raw[:].rearrange("p (b m t) -> p b t m", b=2, t=PACK)[:, b],
            )
        v2_words = gather_bytes(tab2_tile, credit_list[:], U32, "v2_words")

        h1 = {(b, t): keep.tile([P, S], F32, name="h1_%d%d" % (b, t)) for b in range(2) for t in range(PACK)}
        z2_rows = [keep.tile([P, PACK, C], BF16, name="z2_rows%d" % b) for b in range(2)]
        h2, z1_q, w4_q, z2_q, spent, y_banks = {}, {}, {}, {}, {}, {}

        def doc_features(b, t, half):
            rows = slice(P * t, P * (t + 1))
            cols = slice(BANK * half, BANK * (half + 1))
            bank = take_h_bank()
            for a in range(2):
                codes, plane = w1_q[a, b]
                nc.tensor.matmul_mx(
                    bank[:], codes[:, rows].bitcast(FP8X4), plane[:, rows],
                    v_words[a, half][:].bitcast(FP8X4), v_plane[4 * a : P, cols],
                    start=(a == 0), stop=(a == 1),
                )
            nc.scalar.copy(h1[b, t][:, cols], bank[:])

        def credit_features(b, t):
            col = PASS * b + P * t
            bank = take_h_bank()
            nc.tensor.matmul_mx(
                bank[:], w2_codes[:, 2 * col : 2 * (col + P)].bitcast(FP4X4), w2_plane[:, col : col + P],
                v2_words[:].bitcast(FP8X4), v2_plane[:], start=True, stop=True,
            )
            h2[b, t] = take_h2()
            nc.scalar.copy(h2[b, t][:], bank[:])

        def pair_credits(b):
            sums = woven_then_sums[:].bitcast(F32).rearrange("p (side c) -> p side c", side=2)
            for step in range(PACK + 1):
                if step < PACK:
                    nc.vector.tensor_tensor(sums[:, step % 2, :], h1[b, step][:].indirect(pair_list[:]), h2[b, step][:], ADD)
                if step > 0:
                    t = step - 1
                    nc.vector.scalar_tensor_tensor(z2_rows[b][:, t, :], sums[:, t % 2, :], g2[:, b, t : t + 1], h2[b, t][:], MULT, MULT)

        def square_on_scalar(rows, b, cols):
            for t in range(PACK):
                nc.scalar.activation(squares[:, t, :], h1[b, t][:, cols], SQUARE)
            for t in range(PACK):
                nc.scalar.activation(rows[:, t, :], squares[:, t, :], COPY, scale=g1[:, b, t : t + 1])

        def square_on_vector(rows, b, cols):
            for t in range(PACK):
                values = h1[b, t][:, cols]
                nc.vector.scalar_tensor_tensor(rows[:, t, :], values, g1[:, b, t : t + 1], values, MULT, MULT)

        def quantise_z1(c, b, square=square_on_scalar):
            rows = take_z1_rows()
            square(rows, b, slice(CHUNK * c, CHUNK * (c + 1)))
            z1_q[c, b] = quantise(weave(rows, take_z1_woven()), "z1_%d%d" % (c, b))
            spent[c, b] = rows[:].rearrange("p t c -> p (t c)").bitcast(F32)

        def quantise_w4(b):
            w4_q[b] = quantise(weave(w4_raw[b], take_woven()), "w4_%d" % b)

        def quantise_z2(b):
            z2_q[b] = quantise(weave(z2_rows[b], take_woven()), "z2_%d" % b)

        def two_pages(c, pair):
            return ((c, 2 * pair), (c, 2 * pair + 1))

        def two_chunks(c, n):
            return ((c, n), (c + 1, n))

        def score_docs(parts):
            bank = take_y_bank()
            for i, (c, n) in enumerate(parts):
                for b in range(2):
                    codes, plane = z1_q[c, b]
                    nc.tensor.matmul_mx(
                        bank[:, CHUNK * i : CHUNK * (i + 1)], w3_codes[:, b, 2 * P * n : 2 * P * (n + 1)].bitcast(FP4X4),
                        w3_plane[:, N * b + P * n : N * b + P * (n + 1)],
                        codes[:].bitcast(FP8X4), plane[:], start=(b == 0), stop=(b == 1),
                    )
            y_banks[parts] = bank

        def score_credits():
            for n in range(N // P):
                rows = slice(P * n, P * (n + 1))
                bank = take_y_bank()
                for b in range(2):
                    nc.tensor.matmul_mx(
                        bank[:], w4_q[b][0][:, rows].bitcast(FP8X4), w4_q[b][1][:, rows],
                        z2_q[b][0][:].bitcast(FP8X4), z2_q[b][1][:], start=(b == 0), stop=(b == 1),
                    )
                y_banks["credits", n] = bank

        def stage(bank, staged):
            nc.scalar.copy(staged[:], bank[:])
            return staged

        def scatter_docs(n, values, first, count):
            window = pages[n][:].indirect(entries(doc_slots, first, count))
            nc.vector.tensor_tensor(window, values, wg1_tile[:, first : first + count], MULT)

        def place_two_pages(c, pair, staged):
            parts = two_pages(c, pair)
            stage(y_banks[parts], staged)
            for i, (chunk, n) in enumerate(parts):
                scatter_docs(n, staged[:, CHUNK * i : CHUNK * (i + 1)], CHUNK * chunk, CHUNK)

        def place_two_chunks(c, n):
            staged = stage(y_banks[two_chunks(c, n)], take_staged())
            scatter_docs(n, staged[:], CHUNK * c, 2 * CHUNK)

        def place_credits(n, staged):
            stage(y_banks["credits", n], staged)
            nc.vector.tensor_tensor(pages[n][:].indirect(credit_slots[:]), staged[:], wg2_tile[:], MULT)

        def store(n):
            nc.sync.dma_start(out[P * n : P * (n + 1), :], pages[n][:])

        for half in range(S // BANK):
            for t in range(PACK):
                doc_features(0, t, half)
        for t in range(PACK):
            credit_features(0, t)
        quantise_w1(0, 1, nc.vector.tensor_copy, take_woven())
        quantise_w1(1, 1, nc.vector.tensor_copy, woven_then_sums)
        pair_credits(0)
        quantise_z1(0, 0, square_on_vector)

        for t in range(PACK):
            doc_features(1, t, 0)
        quantise_z1(0, 1, square_on_vector)
        for pair in range(2):
            score_docs(two_pages(0, pair))
        for t in range(PACK):
            doc_features(1, t, 1)
            credit_features(1, t)
        quantise_z2(0)
        pair_credits(1)

        place_two_pages(0, 0, take_staged())
        for b in range(2):
            quantise_z1(1, b)
        place_two_pages(0, 1, take_staged())
        for pair in range(2):
            score_docs(two_pages(1, pair))
        quantise_w4(0)
        place_two_pages(1, 0, take_staged())
        quantise_w4(1)
        quantise_z2(1)
        place_two_pages(1, 1, take_staged())
        score_credits()

        quantise_z1(2, 0)
        place_credits(0, take_staged())
        place_credits(1, take_staged())
        quantise_z1(2, 1)
        score_docs(two_pages(2, 0))
        place_credits(2, spent[2, 1])
        quantise_z1(3, 0)
        place_credits(3, spent[3, 0])
        quantise_z1(3, 1)

        place_two_pages(2, 0, spent[3, 1])
        score_docs(two_pages(3, 0))
        for n in (2, 3):
            score_docs(two_chunks(2, n))
        place_two_pages(3, 0, take_staged())
        store(0)
        store(1)
        for n in (2, 3):
            place_two_chunks(2, n)
            store(n)
